import numpy as np, ml_dtypes
CORES = [68,69,70,71,76,77,78,79,84,85,86,87,92,93,94,95]
N = 16
ROOT = 5
def setup_inputs(rng):
    return {"x": rng.standard_normal((N, 128, 64), dtype=np.float32).astype(ml_dtypes.bfloat16)}
def reference(x):
    return {"y": np.broadcast_to(x[ROOT], x.shape)}

@@ -1,0 +1,51 @@
+from concourse.bass import DstId, RemoteDMATransfer
+
+SCRATCH = {
+    "land": ("dram", [128, 64], "bfloat16"),
+}
+SEMAPHORES = ["loaded", "stored", "arrived", "sent"]
+
+ROOT_CORE = 77
+PLAN = {
+    77: [[(94, 0x000F), (90, 0x00F0), (78, 0x0F00), (74, 0xF000)],
+         [(76, 0x00FF), (79, 0xFF00)]],
+    78: [[(68, 0x000F), (69, 0x00F0)]],
+    74: [[(70, 0x000F), (71, 0x00F0)]],
+    94: [[(84, 0x000F), (85, 0x00F0), (92, 0x0F00), (93, 0xF000)]],
+    90: [[(86, 0x000F), (87, 0x00F0), (95, 0xFF00)]],
+}
+
+
+def engines(mask):
+    return bin(mask).count("1")
+
+
+def rank_program(g, core, T, topo):
+    rank = T.rank_of(core)
+    calls = PLAN.get(core, [])
+    if rank is None and not calls:
+        return
+
+    if core == ROOT_CORE:
+        g.dma_start(T.land[:], T.x[:]).then_inc(T.sem.loaded, 16)
+        g.wait_ge(T.sem.loaded, 16)
+    else:
+        need = [engines(m) for cs in PLAN.values() for c in cs for (d, m) in c if d == core]
+        g.wait_ge(T.sem.arrived, need[0])
+
+    sent = 0
+    for call in calls:
+        transfers = []
+        for dst, mask in call:
+            rid, pid, se = topo.addr(dst)
+            transfers.append(RemoteDMATransfer(dst_ids=[DstId(rid=rid, pnc=pid)], dma_engine_mask=mask,
+                                               remote_sem=T.sem.arrived, src=T.land[:], dst=T.land[:]))
+            sent += engines(mask)
+        g.remote_dma_fused(transfers, local_sem=T.sem.sent)
+
+    if rank is not None:
+        src = T.x if core == ROOT_CORE else T.land
+        g.dma_start(T.y[:], src[:]).then_inc(T.sem.stored, 16)
+        g.wait_ge(T.sem.stored, 16)
+    if sent:
+        g.wait_ge(T.sem.sent, sent)

@@ -7,12 +7,12 @@ SEMAPHORES = ["loaded", "stored", "arrived", "sent"]
 
 ROOT_CORE = 77
 PLAN = {
-    77: [[(94, 0x000F), (90, 0x00F0), (78, 0x0F00), (74, 0xF000)],
-         [(76, 0x00FF), (79, 0xFF00)]],
-    78: [[(68, 0x000F), (69, 0x00F0)]],
-    74: [[(70, 0x000F), (71, 0x00F0)]],
-    94: [[(84, 0x000F), (85, 0x00F0), (92, 0x0F00), (93, 0xF000)]],
-    90: [[(86, 0x000F), (87, 0x00F0), (95, 0xFF00)]],
+    77: [[((94, 90), 0x00FF), ((78, 74), 0xFF00)],
+         [((76, 79), 0xFFFF)]],
+    78: [[((68, 69), 0x00FF)]],
+    74: [[((70, 71), 0x00FF)]],
+    94: [[((84, 85), 0x00FF), ((92, 93), 0xFF00)]],
+    90: [[((86, 87), 0x00FF), ((95,), 0xFF00)]],
 }
 
 
@@ -30,16 +30,19 @@ def rank_program(g, core, T, topo):
         g.dma_start(T.land[:], T.x[:]).then_inc(T.sem.loaded, 16)
         g.wait_ge(T.sem.loaded, 16)
     else:
-        need = [engines(m) for cs in PLAN.values() for c in cs for (d, m) in c if d == core]
+        need = [engines(m) for cs in PLAN.values() for c in cs for (ds, m) in c if core in ds]
         g.wait_ge(T.sem.arrived, need[0])
 
     sent = 0
     for call in calls:
         transfers = []
-        for dst, mask in call:
-            rid, pid, se = topo.addr(dst)
-            transfers.append(RemoteDMATransfer(dst_ids=[DstId(rid=rid, pnc=pid)], dma_engine_mask=mask,
-                                               remote_sem=T.sem.arrived, src=T.land[:], dst=T.land[:]))
+        for dsts, mask in call:
+            ids = []
+            for d in dsts:
+                rid, pid, se = topo.addr(d)
+                ids.append(DstId(rid=rid, pnc=pid))
+            transfers.append(RemoteDMATransfer(dst_ids=ids, dma_engine_mask=mask, remote_sem=T.sem.arrived,
+                                               srcs=[T.land[:]], dsts=[T.land[:] for d in dsts]))
             sent += engines(mask)
         g.remote_dma_fused(transfers, local_sem=T.sem.sent)
 

from concourse.bass import DstId, RemoteDMATransfer

SCRATCH = {
    "land": ("dram", [128, 64], "bfloat16"),
}
SEMAPHORES = ["loaded", "stored", "arrived", "sent"]

ROOT_CORE = 77
PLAN = {
    77: [[((94, 90), 0x00FF), ((78, 74), 0xFF00)],
         [((76, 79), 0xFFFF)]],
    78: [[((68, 69), 0x00FF)]],
    74: [[((70, 71), 0x00FF)]],
    94: [[((84, 85), 0x00FF), ((92, 93), 0xFF00)]],
    90: [[((86, 87), 0x00FF), ((95,), 0xFF00)]],
}


def engines(mask):
    return bin(mask).count("1")


def rank_program(g, core, T, topo):
    rank = T.rank_of(core)
    calls = PLAN.get(core, [])
    if rank is None and not calls:
        return

    if core == ROOT_CORE:
        g.dma_start(T.land[:], T.x[:]).then_inc(T.sem.loaded, 16)
        g.wait_ge(T.sem.loaded, 16)
    else:
        need = [engines(m) for cs in PLAN.values() for c in cs for (ds, m) in c if core in ds]
        g.wait_ge(T.sem.arrived, need[0])

    sent = 0
    for call in calls:
        transfers = []
        for dsts, mask in call:
            ids = []
            for d in dsts:
                rid, pid, se = topo.addr(d)
                ids.append(DstId(rid=rid, pnc=pid))
            transfers.append(RemoteDMATransfer(dst_ids=ids, dma_engine_mask=mask, remote_sem=T.sem.arrived,
                                               srcs=[T.land[:]], dsts=[T.land[:] for d in dsts]))
            sent += engines(mask)
        g.remote_dma_fused(transfers, local_sem=T.sem.sent)

    if rank is not None:
        src = T.x if core == ROOT_CORE else T.land
        g.dma_start(T.y[:], src[:]).then_inc(T.sem.stored, 16)
        g.wait_ge(T.sem.stored, 16)
    if sent:
        g.wait_ge(T.sem.sent, sent)
